import numpy as np
import ml_dtypes

BF16 = ml_dtypes.bfloat16


def bf(x):
    return np.asarray(x, np.float32).astype(BF16)


def f32(x):
    return np.asarray(x, np.float32)


def f64(x):
    return np.asarray(x).astype(np.float64)


def striped(idx):
    return np.tile(idx.reshape(-1, 16).T, (8, 1))


def rows(idx, k):
    return np.tile(idx, (k, 1))


def look(tab, idx):
    return np.take_along_axis(f64(tab), rows(idx, len(tab)), axis=1)


K, S, V, N = 128, 2048, 2048, 2048


def setup_inputs():
    return {"tab": f32(np.random.standard_normal((2, K, S))), "th": f32(0.5 * np.random.standard_normal((K, V))), "offs": striped(np.random.permutation(S)[:N])}


def reference(tab, th, offs):
    idx = offs[:16].T.reshape(-1)
    x = (look(tab[0], idx) >= f64(th)) * look(tab[1], idx)
    return x

@@ -1,0 +1,57 @@
+import concourse.mybir as mybir
+
+F32 = mybir.dt.float32
+U16 = mybir.dt.uint16
+is_ge = mybir.AluOpType.is_ge
+mult = mybir.AluOpType.mult
+
+ROWS = 128
+PLACES = 2048
+ENTRIES = 2048
+COLUMN = 16
+SHORTEST = 128
+
+
+def growing_pieces():
+    pieces = [(0, SHORTEST)]
+    while pieces[-1][1] < ENTRIES:
+        done = pieces[-1][1]
+        pieces.append((done, 2 * done))
+    return pieces
+
+
+def shrinking_pieces():
+    return [(ENTRIES - stop, ENTRIES - start) for start, stop in reversed(growing_pieces())]
+
+
+def tile_lookup_sel_out_kernel(tc, tab, th, offs, out):
+    nc = tc.nc
+    with tc.tile_pool(name="held", bufs=1) as held:
+        offsets = held.tile([ROWS, ENTRIES // COLUMN], U16)
+        keys = held.tile([ROWS, PLACES], F32)
+        values = held.tile([ROWS, PLACES], F32)
+        thresholds = held.tile([ROWS, ENTRIES], F32)
+        reached = held.tile([ROWS, ENTRIES], F32)
+        picked = held.tile([ROWS, ENTRIES], F32)
+
+        nc.sync.dma_start(offsets[:], offs)
+        half = PLACES // 2
+        nc.sync.dma_start(keys[:, :half], tab[0, :, :half])
+        nc.scalar.dma_start(keys[:, half:], tab[0, :, half:])
+        for start, stop in growing_pieces():
+            nc.sync.dma_start(thresholds[:, start:stop], th[:, start:stop])
+        nc.sync.dma_start(values[:], tab[1])
+
+        def listed(start, stop):
+            return offsets[:, start // COLUMN : stop // COLUMN]
+
+        for start, stop in growing_pieces():
+            nc.vector.tensor_tensor(
+                reached[:, start:stop], keys[:].indirect(listed(start, stop)), thresholds[:, start:stop], is_ge
+            )
+
+        for start, stop in shrinking_pieces():
+            nc.vector.tensor_tensor(
+                picked[:, start:stop], values[:].indirect(listed(start, stop)), reached[:, start:stop], mult
+            )
+            nc.scalar.dma_start(out[:, start:stop], picked[:, start:stop])

@@ -10,22 +10,22 @@ PLACES = 2048
 ENTRIES = 2048
 COLUMN = 16
 SHORTEST = 128
+SYNC_KEYS = 896
 
 
-def growing_pieces():
-    pieces = [(0, SHORTEST)]
-    while pieces[-1][1] < ENTRIES:
-        done = pieces[-1][1]
-        pieces.append((done, 2 * done))
-    return pieces
-
-
-def shrinking_pieces():
-    return [(ENTRIES - stop, ENTRIES - start) for start, stop in reversed(growing_pieces())]
+def doubling_cuts():
+    cuts = [0, SHORTEST]
+    while cuts[-1] < ENTRIES:
+        cuts.append(2 * cuts[-1])
+    return cuts
 
 
 def tile_lookup_sel_out_kernel(tc, tab, th, offs, out):
     nc = tc.nc
+    cuts = doubling_cuts()
+    growing = [slice(start, stop) for start, stop in zip(cuts, cuts[1:])]
+    shrinking = [slice(ENTRIES - piece.stop, ENTRIES - piece.start) for piece in reversed(growing)]
+
     with tc.tile_pool(name="held", bufs=1) as held:
         offsets = held.tile([ROWS, ENTRIES // COLUMN], U16)
         keys = held.tile([ROWS, PLACES], F32)
@@ -35,23 +35,18 @@ def tile_lookup_sel_out_kernel(tc, tab, th, offs, out):
         picked = held.tile([ROWS, ENTRIES], F32)
 
         nc.sync.dma_start(offsets[:], offs)
-        half = PLACES // 2
-        nc.sync.dma_start(keys[:, :half], tab[0, :, :half])
-        nc.scalar.dma_start(keys[:, half:], tab[0, :, half:])
-        for start, stop in growing_pieces():
-            nc.sync.dma_start(thresholds[:, start:stop], th[:, start:stop])
+        nc.sync.dma_start(keys[:, :SYNC_KEYS], tab[0, :, :SYNC_KEYS])
+        nc.scalar.dma_start(keys[:, SYNC_KEYS:], tab[0, :, SYNC_KEYS:])
+        for piece in growing:
+            nc.sync.dma_start(thresholds[:, piece], th[:, piece])
         nc.sync.dma_start(values[:], tab[1])
 
-        def listed(start, stop):
-            return offsets[:, start // COLUMN : stop // COLUMN]
+        def listed(piece):
+            return offsets[:, piece.start // COLUMN : piece.stop // COLUMN]
 
-        for start, stop in growing_pieces():
-            nc.vector.tensor_tensor(
-                reached[:, start:stop], keys[:].indirect(listed(start, stop)), thresholds[:, start:stop], is_ge
-            )
+        for piece in growing:
+            nc.vector.tensor_tensor(reached[:, piece], keys[:].indirect(listed(piece)), thresholds[:, piece], is_ge)
 
-        for start, stop in shrinking_pieces():
-            nc.vector.tensor_tensor(
-                picked[:, start:stop], values[:].indirect(listed(start, stop)), reached[:, start:stop], mult
-            )
-            nc.scalar.dma_start(out[:, start:stop], picked[:, start:stop])
+        for piece in shrinking:
+            nc.vector.tensor_tensor(picked[:, piece], values[:].indirect(listed(piece)), reached[:, piece], mult)
+            nc.scalar.dma_start(out[:, piece], picked[:, piece])

@@ -10,6 +10,7 @@ PLACES = 2048
 ENTRIES = 2048
 COLUMN = 16
 SHORTEST = 128
+SOONER = 64
 SYNC_KEYS = 896
 
 
@@ -20,11 +21,16 @@ def doubling_cuts():
     return cuts
 
 
+def pieces(cuts):
+    return [slice(start, stop) for start, stop in zip(cuts, cuts[1:])]
+
+
 def tile_lookup_sel_out_kernel(tc, tab, th, offs, out):
     nc = tc.nc
     cuts = doubling_cuts()
-    growing = [slice(start, stop) for start, stop in zip(cuts, cuts[1:])]
-    shrinking = [slice(ENTRIES - piece.stop, ENTRIES - piece.start) for piece in reversed(growing)]
+    growing = pieces(cuts)
+    halving = [ENTRIES - cut for cut in reversed(cuts)]
+    shrinking = pieces(halving[:1] + [cut - SOONER for cut in halving[1:-2]] + halving[-2:])
 
     with tc.tile_pool(name="held", bufs=1) as held:
         offsets = held.tile([ROWS, ENTRIES // COLUMN], U16)

@@ -11,7 +11,6 @@ ENTRIES = 2048
 COLUMN = 16
 SHORTEST = 128
 SOONER = 64
-SYNC_KEYS = 896
 
 
 def doubling_cuts():
@@ -40,10 +39,10 @@ def tile_lookup_sel_out_kernel(tc, tab, th, offs, out):
         reached = held.tile([ROWS, ENTRIES], F32)
         picked = held.tile([ROWS, ENTRIES], F32)
 
+        nc.sync.dma_start(keys[:], tab[0])
+        nc.scalar.dma_start(thresholds[:, growing[0]], th[:, growing[0]])
         nc.sync.dma_start(offsets[:], offs)
-        nc.sync.dma_start(keys[:, :SYNC_KEYS], tab[0, :, :SYNC_KEYS])
-        nc.scalar.dma_start(keys[:, SYNC_KEYS:], tab[0, :, SYNC_KEYS:])
-        for piece in growing:
+        for piece in growing[1:]:
             nc.sync.dma_start(thresholds[:, piece], th[:, piece])
         nc.sync.dma_start(values[:], tab[1])
 

@@ -27,7 +27,7 @@ def pieces(cuts):
 def tile_lookup_sel_out_kernel(tc, tab, th, offs, out):
     nc = tc.nc
     cuts = doubling_cuts()
-    growing = pieces(cuts)
+    growing = pieces([0, SHORTEST // 2, 3 * SHORTEST // 2, 7 * SHORTEST // 2, ENTRIES // 2, ENTRIES])
     halving = [ENTRIES - cut for cut in reversed(cuts)]
     shrinking = pieces(halving[:1] + [cut - SOONER for cut in halving[1:-2]] + halving[-2:])
 

@@ -44,7 +44,8 @@ def tile_lookup_sel_out_kernel(tc, tab, th, offs, out):
         nc.sync.dma_start(offsets[:], offs)
         for piece in growing[1:]:
             nc.sync.dma_start(thresholds[:, piece], th[:, piece])
-        nc.sync.dma_start(values[:], tab[1])
+        for part in pieces([0, PLACES // 2, 3 * PLACES // 4, PLACES]):
+            nc.sync.dma_start(values[:, part], tab[1, :, part])
 
         def listed(piece):
             return offsets[:, piece.start // COLUMN : piece.stop // COLUMN]

@@ -44,7 +44,7 @@ def tile_lookup_sel_out_kernel(tc, tab, th, offs, out):
         nc.sync.dma_start(offsets[:], offs)
         for piece in growing[1:]:
             nc.sync.dma_start(thresholds[:, piece], th[:, piece])
-        for part in pieces([0, PLACES // 2, 3 * PLACES // 4, PLACES]):
+        for part in pieces(range(0, PLACES + 1, PLACES // 4)):
             nc.sync.dma_start(values[:, part], tab[1, :, part])
 
         def listed(piece):

@@ -11,6 +11,7 @@ ENTRIES = 2048
 COLUMN = 16
 SHORTEST = 128
 SOONER = 64
+BURST = 256
 
 
 def doubling_cuts():
@@ -32,12 +33,12 @@ def tile_lookup_sel_out_kernel(tc, tab, th, offs, out):
     shrinking = pieces(halving[:1] + [cut - SOONER for cut in halving[1:-2]] + halving[-2:])
 
     with tc.tile_pool(name="held", bufs=1) as held:
-        offsets = held.tile([ROWS, ENTRIES // COLUMN], U16)
-        keys = held.tile([ROWS, PLACES], F32)
-        values = held.tile([ROWS, PLACES], F32)
-        thresholds = held.tile([ROWS, ENTRIES], F32)
-        reached = held.tile([ROWS, ENTRIES], F32)
-        picked = held.tile([ROWS, ENTRIES], F32)
+        offsets = held.tile([ROWS, ENTRIES // COLUMN], U16, align_bytes=BURST)
+        keys = held.tile([ROWS, PLACES], F32, align_bytes=BURST)
+        values = held.tile([ROWS, PLACES], F32, align_bytes=BURST)
+        thresholds = held.tile([ROWS, ENTRIES], F32, align_bytes=BURST)
+        reached = held.tile([ROWS, ENTRIES], F32, align_bytes=BURST)
+        picked = held.tile([ROWS, ENTRIES], F32, align_bytes=BURST)
 
         nc.sync.dma_start(keys[:], tab[0])
         nc.scalar.dma_start(thresholds[:, growing[0]], th[:, growing[0]])

@@ -9,16 +9,8 @@ ROWS = 128
 PLACES = 2048
 ENTRIES = 2048
 COLUMN = 16
-SHORTEST = 128
-SOONER = 64
+SHORTEST = 64
 BURST = 256
-
-
-def doubling_cuts():
-    cuts = [0, SHORTEST]
-    while cuts[-1] < ENTRIES:
-        cuts.append(2 * cuts[-1])
-    return cuts
 
 
 def pieces(cuts):
@@ -27,10 +19,8 @@ def pieces(cuts):
 
 def tile_lookup_sel_out_kernel(tc, tab, th, offs, out):
     nc = tc.nc
-    cuts = doubling_cuts()
-    growing = pieces([0, SHORTEST // 2, 3 * SHORTEST // 2, 7 * SHORTEST // 2, ENTRIES // 2, ENTRIES])
-    halving = [ENTRIES - cut for cut in reversed(cuts)]
-    shrinking = pieces(halving[:1] + [cut - SOONER for cut in halving[1:-2]] + halving[-2:])
+    growing = pieces([0, SHORTEST, 3 * SHORTEST, 7 * SHORTEST, ENTRIES // 2, ENTRIES])
+    shrinking = pieces([0, *(ENTRIES - (ENTRIES >> halvings) for halvings in range(1, 5)), ENTRIES])
 
     with tc.tile_pool(name="held", bufs=1) as held:
         offsets = held.tile([ROWS, ENTRIES // COLUMN], U16, align_bytes=BURST)

@@ -10,6 +10,7 @@ PLACES = 2048
 ENTRIES = 2048
 COLUMN = 16
 SHORTEST = 64
+LINE = 128
 BURST = 256
 
 
@@ -19,7 +20,9 @@ def pieces(cuts):
 
 def tile_lookup_sel_out_kernel(tc, tab, th, offs, out):
     nc = tc.nc
-    growing = pieces([0, SHORTEST, 3 * SHORTEST, 7 * SHORTEST, ENTRIES // 2, ENTRIES])
+    middle = ENTRIES // 2
+    doubling = pieces([middle - 3 * LINE - SHORTEST, middle - 3 * LINE, middle - 2 * LINE, middle])
+    growing = [*doubling, slice(0, doubling[0].start), slice(middle, ENTRIES)]
     shrinking = pieces([0, *(ENTRIES - (ENTRIES >> halvings) for halvings in range(1, 5)), ENTRIES])
 
     with tc.tile_pool(name="held", bufs=1) as held:

@@ -9,9 +9,10 @@ ROWS = 128
 PLACES = 2048
 ENTRIES = 2048
 COLUMN = 16
-SHORTEST = 64
-LINE = 128
 BURST = 256
+COMPARED = (0, 64, 192, 448, 1024, ENTRIES)
+MULTIPLIED = (0, 768, 1408, 1728, 1920, ENTRIES)
+FIRST_STORES = 4
 
 
 def pieces(cuts):
@@ -20,10 +21,8 @@ def pieces(cuts):
 
 def tile_lookup_sel_out_kernel(tc, tab, th, offs, out):
     nc = tc.nc
-    middle = ENTRIES // 2
-    doubling = pieces([middle - 3 * LINE - SHORTEST, middle - 3 * LINE, middle - 2 * LINE, middle])
-    growing = [*doubling, slice(0, doubling[0].start), slice(middle, ENTRIES)]
-    shrinking = pieces([0, *(ENTRIES - (ENTRIES >> halvings) for halvings in range(1, 5)), ENTRIES])
+    growing = pieces(COMPARED)
+    shrinking = pieces(MULTIPLIED)
 
     with tc.tile_pool(name="held", bufs=1) as held:
         offsets = held.tile([ROWS, ENTRIES // COLUMN], U16, align_bytes=BURST)
@@ -38,8 +37,7 @@ def tile_lookup_sel_out_kernel(tc, tab, th, offs, out):
         nc.sync.dma_start(offsets[:], offs)
         for piece in growing[1:]:
             nc.sync.dma_start(thresholds[:, piece], th[:, piece])
-        for part in pieces(range(0, PLACES + 1, PLACES // 4)):
-            nc.sync.dma_start(values[:, part], tab[1, :, part])
+        nc.sync.dma_start(values[:], tab[1])
 
         def listed(piece):
             return offsets[:, piece.start // COLUMN : piece.stop // COLUMN]
@@ -47,6 +45,15 @@ def tile_lookup_sel_out_kernel(tc, tab, th, offs, out):
         for piece in growing:
             nc.vector.tensor_tensor(reached[:, piece], keys[:].indirect(listed(piece)), thresholds[:, piece], is_ge)
 
-        for piece in shrinking:
+        def multiply(piece):
             nc.vector.tensor_tensor(picked[:, piece], values[:].indirect(listed(piece)), reached[:, piece], mult)
+
+        first = shrinking[0]
+        multiply(first)
+        lead, *rest = pieces(range(first.start, first.stop + 1, first.stop // FIRST_STORES))
+        nc.scalar.dma_start(out[:, lead], picked[:, lead])
+        for part in rest:
+            nc.sync.dma_start(out[:, part], picked[:, part])
+        for piece in shrinking[1:]:
+            multiply(piece)
             nc.scalar.dma_start(out[:, piece], picked[:, piece])

@@ -10,7 +10,7 @@ PLACES = 2048
 ENTRIES = 2048
 COLUMN = 16
 BURST = 256
-COMPARED = (0, 64, 192, 448, 1024, ENTRIES)
+COMPARED = (0, 64, 256, 512, 1024, ENTRIES)
 MULTIPLIED = (0, 768, 1408, 1728, 1920, ENTRIES)
 FIRST_STORES = 4
 

import concourse.mybir as mybir

F32 = mybir.dt.float32
U16 = mybir.dt.uint16
is_ge = mybir.AluOpType.is_ge
mult = mybir.AluOpType.mult

ROWS = 128
PLACES = 2048
ENTRIES = 2048
COLUMN = 16
BURST = 256
COMPARED = (0, 64, 256, 512, 1024, ENTRIES)
MULTIPLIED = (0, 768, 1408, 1728, 1920, ENTRIES)
FIRST_STORES = 4


def pieces(cuts):
    return [slice(start, stop) for start, stop in zip(cuts, cuts[1:])]


def tile_lookup_sel_out_kernel(tc, tab, th, offs, out):
    nc = tc.nc
    growing = pieces(COMPARED)
    shrinking = pieces(MULTIPLIED)

    with tc.tile_pool(name="held", bufs=1) as held:
        offsets = held.tile([ROWS, ENTRIES // COLUMN], U16, align_bytes=BURST)
        keys = held.tile([ROWS, PLACES], F32, align_bytes=BURST)
        values = held.tile([ROWS, PLACES], F32, align_bytes=BURST)
        thresholds = held.tile([ROWS, ENTRIES], F32, align_bytes=BURST)
        reached = held.tile([ROWS, ENTRIES], F32, align_bytes=BURST)
        picked = held.tile([ROWS, ENTRIES], F32, align_bytes=BURST)

        nc.sync.dma_start(keys[:], tab[0])
        nc.scalar.dma_start(thresholds[:, growing[0]], th[:, growing[0]])
        nc.sync.dma_start(offsets[:], offs)
        for piece in growing[1:]:
            nc.sync.dma_start(thresholds[:, piece], th[:, piece])
        nc.sync.dma_start(values[:], tab[1])

        def listed(piece):
            return offsets[:, piece.start // COLUMN : piece.stop // COLUMN]

        for piece in growing:
            nc.vector.tensor_tensor(reached[:, piece], keys[:].indirect(listed(piece)), thresholds[:, piece], is_ge)

        def multiply(piece):
            nc.vector.tensor_tensor(picked[:, piece], values[:].indirect(listed(piece)), reached[:, piece], mult)

        first = shrinking[0]
        multiply(first)
        lead, *rest = pieces(range(first.start, first.stop + 1, first.stop // FIRST_STORES))
        nc.scalar.dma_start(out[:, lead], picked[:, lead])
        for part in rest:
            nc.sync.dma_start(out[:, part], picked[:, part])
        for piece in shrinking[1:]:
            multiply(piece)
            nc.scalar.dma_start(out[:, piece], picked[:, piece])
